import numpy as np
import ml_dtypes


def mxq(x, axis, fmt="e4m3"):
    dtype, down = {"e4m3": (ml_dtypes.float8_e4m3fn, 7), "e5m2": (ml_dtypes.float8_e5m2, 14)}[fmt]
    v = np.moveaxis(np.asarray(x, np.float32).astype(ml_dtypes.bfloat16).astype(np.float64), axis, -1)
    blocks = v.reshape(v.shape[:-1] + (-1, 32))
    amax = np.abs(blocks).max(-1, keepdims=True)
    byte = np.maximum(np.where(amax > 0, np.frexp(amax)[1] - 1 + 127, 0) - down, 1)
    scale = np.exp2(byte - 127.0)
    codes = (blocks / scale).astype(np.float32).astype(dtype).astype(np.float64)
    return np.moveaxis((codes * scale).reshape(v.shape), -1, axis)


WIDE = False


def mx_kscale(k):
    if not WIDE:
        return np.ones(k)
    levels = np.array([10, -10, 5, -5, 0])
    if k % 512:
        return np.exp2(np.random.permutation(np.resize(levels, k // 32))).repeat(32)
    a = np.empty((k // 512, 16))
    for p in range(k // 512):
        a[p, :8] = np.random.permutation(np.resize(levels, 8))
        for g in range(8):
            far = levels[np.abs(levels - a[p, g]) >= 10]
            a[p, g + 8] = far[np.random.randint(len(far))]
    return np.exp2(a.ravel()).repeat(32)


def f64(x):
    return np.asarray(x).astype(np.float64)


def striped(idx):
    return np.tile(idx.reshape(-1, 16).T, (8, 1)).astype(np.uint16)


def unstriped(offs):
    return offs[:16].T.reshape(-1).astype(np.int64)


def silu(v):
    return v / (1.0 + np.exp(-np.maximum(v, -700.0)))


K, T, S, H, N = 512, 1024, 512, 512, 256
P = 2 ** 7


def setup_inputs():
    n = np.random.standard_normal
    s = mx_kscale(K)[:, None]
    u = mx_kscale(H)
    return {
        "xT": (n((K, T)) * s).astype(np.float32),
        "gate": np.tile(np.random.uniform(0.2, 1.0, T), (P, 1)).astype(np.float32),
        "w1": (n((K, H)) / np.sqrt(K) / s * u).astype(np.float32),
        "w2": (n((H, N)) / np.sqrt(H) / u[:, None]).astype(np.float32),
        "offs": striped(np.random.permutation(T)[:S]),
    }


def reference(xT, gate, w1, w2, offs):
    xq = mxq(f64(xT)[:, unstriped(offs)], 0, "e4m3")
    h = silu(mxq(f64(w1), 0, "e4m3").T @ xq)
    y = mxq(f64(w2), 0, "e4m3").T @ mxq(h, 0, "e4m3")
    g = f64(gate)[:1][:, unstriped(offs)]
    out = np.zeros((N, T))
    out[:, unstriped(offs)] = y * g
    return out

@@ -1,0 +1,186 @@
+from contextlib import ExitStack
+
+import concourse.mybir as mybir
+from concourse.masks import make_identity
+
+K, T, S, H, N = 512, 1024, 512, 512, 256
+FLOPS = 2 * S * (K * H + H * N)
+
+F32 = mybir.dt.float32
+BF16 = mybir.dt.bfloat16
+U32 = mybir.dt.uint32
+U16 = mybir.dt.uint16
+U8 = mybir.dt.uint8
+FP8X4 = mybir.dt.float8_e4m3fn_x4
+ACT = mybir.ActivationFunctionType
+MULT = mybir.AluOpType.mult
+
+P = 128
+PACK = 4
+CHUNK = 128
+LIST_COLS = 16
+
+
+def tile_picked_modgate_mlpsilu_l_kernel(tc, xT, gate, w1, w2, offs, out):
+    nc = tc.nc
+    with ExitStack() as ctx:
+        keep = ctx.enter_context(tc.tile_pool(name="keep", bufs=1))
+        shared = ctx.enter_context(tc.tile_pool(name="shared", bufs=1))
+        psum = ctx.enter_context(tc.psum_pool(name="psum", bufs=4))
+
+        def entries(lo, hi):
+            return offsets[:, lo // LIST_COLS : hi // LIST_COLS]
+
+        def quantize(codes, scales, values):
+            nc.vector.quantize_mx(out=codes.bitcast(FP8X4), scales=scales, in_=values)
+
+        def product(acc, w_codes, w_scales, a_codes, a_scales):
+            nc.tensor.matmul_mx(out=acc, lhsT=w_codes.bitcast(FP8X4), lhsT_scale=w_scales,
+                                rhs=a_codes.bitcast(FP8X4), rhs_scale=a_scales, start=True, stop=True)
+
+        gate_row = keep.tile([P, 2, PACK], F32)
+        nc.sync.dma_start(out=gate_row[:], in_=gate[0:1, :].rearrange("o (h p m) -> (o p) h m", h=2, p=P))
+        x_rows = xT.rearrange("(p j) t -> p j t", j=PACK)
+        x_pieces = [[0,0,512],[0,512,1024],[1,0,512],[1,512,1024]]
+        x_raw = []
+        offsets = keep.tile([P, S // LIST_COLS], U16)
+        for i, (u, lo, hi) in enumerate(x_pieces):
+            raw = keep.tile([P, 2, hi - lo], F32, name="x_raw%d" % i, tag="x_raw%d" % i, align_bytes=64)
+            nc.sync.dma_start(out=raw[:], in_=x_rows[:, 2 * u : 2 * u + 2, lo:hi])
+            x_raw.append(raw)
+            if i == 0:
+                nc.sync.dma_start(offsets[:], offs)
+        w1_rows = w1.rearrange("(p j) c -> p j c", j=PACK)
+        w1_raw = []
+        for h in range(2):
+            raw = keep.tile([P, PACK, H // 2], F32, name="w1_raw%d" % h, tag="w1_raw%d" % h, align_bytes=64)
+            nc.sync.dma_start(out=raw[:], in_=w1_rows[:, :, h * (H // 2) : (h + 1) * (H // 2)])
+            w1_raw.append(raw)
+        w2_raw = keep.tile([P, PACK, N], F32)
+        nc.sync.dma_start(out=w2_raw[:], in_=w2.rearrange("(p j) n -> p j n", j=PACK))
+
+        ident = keep.tile([P, P], F32)
+        make_identity(nc, ident[:])
+        warm = keep.tile([P, 1], F32)
+        nc.scalar.activation(warm[:], ident[:, 0:1], ACT.Silu)
+        windows = [keep.tile([P, T], F32, name="window%d" % b) for b in range(N // P)]
+        for window in windows:
+            nc.vector.memset(window[:], 0.0)
+
+        gate_all = shared.tile([P, T], F32, offset=2048, align_bytes=64)
+        gate_view = gate_all[:].rearrange("q (h p m) -> q h p m", h=2, m=PACK)
+        for half in range(2):
+            bank = psum.tile([P, PACK, P], F32, tag="small", name="gate_bank")
+            for m in range(PACK):
+                nc.tensor.transpose(bank[:, m, :], gate_row[:, half, m : m + 1].to_broadcast([P, P]), ident[:])
+            nc.vector.tensor_copy(gate_view[:, half], bank[:].rearrange("q m p -> q p m"))
+
+        gate_picked = keep.tile([P, S], F32)
+        nc.vector.tensor_copy(gate_picked[:], gate_all[:].indirect(offsets[:]))
+
+        x_pairs = [keep.tile([P, T, 2], BF16, name="x_pairs0"), shared.tile([P, T, 2], BF16, name="x_pairs1", offset=0, align_bytes=64)]
+        groups = [[0,128],[128,256],[256,512]]
+        picked = shared.tile([P, S, 2], U32, offset=4096, align_bytes=64)
+        x_codes = [keep.tile([P, CHUNK], U32, align_bytes=64, name="x_codes_first")]
+        x_scales = keep.tile([P, S], U8, align_bytes=64)
+
+        def cast(i, vector_cols):
+            u, lo, hi = x_pieces[i]
+            src = x_raw[i][:].rearrange("p e t -> p t e")
+            if vector_cols > 0:
+                nc.vector.tensor_copy(x_pairs[u][:, lo : lo + vector_cols, :], src[:, :vector_cols, :])
+            if vector_cols < hi - lo:
+                nc.scalar.copy(x_pairs[u][:, lo + vector_cols : hi, :], src[:, vector_cols:, :])
+
+        def gather(u):
+            window = x_pairs[u][:].rearrange("p t e -> p (t e)").bitcast(U32)
+            nc.vector.tensor_copy(picked[:, :, u], window.indirect(offsets[:]))
+
+        def x_words(lo, hi):
+            return x_codes[0][:, lo:hi] if hi <= CHUNK else x_codes[1][:, lo - CHUNK : hi - CHUNK]
+
+        def quantize_x(g):
+            lo, hi = groups[g]
+            quantize(x_words(lo, hi), x_scales[:, lo:hi], picked[:, lo:hi, :].rearrange("p s u -> p (s u)").bitcast(BF16))
+
+        shares = [0,0,0,320]
+        for i, (u, lo, hi) in enumerate(x_pieces):
+            cast(i, shares[i])
+            if hi == T:
+                gather(u)
+        quantize_x(0)
+
+        half = P // 2
+        w1_grouped = [
+            keep.tile([P, PACK, half, PACK], BF16, align_bytes=64, name="w1_grouped0", tag="x_raw3"),
+            shared.tile([P, PACK, half, PACK], BF16, align_bytes=64, name="w1_grouped1", offset=0),
+        ]
+        w1_codes = shared.tile([P, H], U32, align_bytes=64, offset=2048)
+        w1_scales = keep.tile([P, H], U8, align_bytes=64)
+        for h, copy in enumerate((nc.scalar.copy, nc.vector.tensor_copy)):
+            copy(w1_grouped[h][:].rearrange("p t m j -> p m j t"), w1_raw[h][:].rearrange("p j (m t) -> p m j t", t=PACK))
+        for t in range(PACK):
+            for h in range(2):
+                cols = slice(t * P + h * half, t * P + (h + 1) * half)
+                quantize(w1_codes[:, cols], w1_scales[:, cols], w1_grouped[h][:, t].rearrange("p m j -> p (m j)"))
+        x_codes.append(keep.tile([P, S - CHUNK], U32, align_bytes=64, name="x_codes_rest", tag="w1_raw1"))
+        for g in range(1, len(groups)):
+            quantize_x(g)
+
+        w2_codes = keep.tile([P, N], U32, align_bytes=64)
+        w2_scales = keep.tile([P, N], U8, align_bytes=64)
+        for b in range(N // P):
+            if b == 0:
+                w2_grouped = shared.tile([P, P, PACK], BF16, align_bytes=64, name="w2_grouped0", offset=0)
+            else:
+                w2_grouped = keep.tile([P, P, PACK], BF16, align_bytes=64, name="w2_grouped1", tag="w1_raw0")
+            (nc.vector.tensor_copy, nc.scalar.copy)[b](w2_grouped[:].rearrange("p (c i) j -> p c j i", i=4),
+                w2_raw[:, :, b * P : (b + 1) * P].rearrange("p j (c i) -> p c j i", i=4))
+            quantize(w2_codes[:, b * P : (b + 1) * P], w2_scales[:, b * P : (b + 1) * P], w2_grouped[:].rearrange("p n j -> p (n j)"))
+
+
+        y_sb = [keep.tile([P, S], F32, name="y_sb%d" % b) for b in range(N // P)]
+        h_codes = keep.tile([P, S], U32, align_bytes=64)
+        h_scales = keep.tile([P, S], U8, align_bytes=64)
+
+        def first_layer(c):
+            cols = slice(c * CHUNK, (c + 1) * CHUNK)
+            bank = psum.tile([P, PACK, CHUNK], F32, tag="hidden", name="h_bank")
+            for t in range(PACK):
+                product(bank[:, t, :], w1_codes[:, t * P : (t + 1) * P], w1_scales[:, t * P : (t + 1) * P], x_words(cols.start, cols.stop), x_scales[:, cols])
+            h_grouped = keep.tile([P, CHUNK, PACK], BF16, align_bytes=64, name="h_grouped%d" % c)
+            nc.scalar.activation(h_grouped[:], bank[:].rearrange("p t s -> p s t"), ACT.Silu)
+            return h_grouped
+
+        def quantize_h(c, h_grouped):
+            cols = slice(c * CHUNK, (c + 1) * CHUNK)
+            quantize(h_codes[:, cols], h_scales[:, cols], h_grouped[:].rearrange("p s t -> p (s t)"))
+
+        def second_layer(b, lo, hi, copy):
+            acc = psum.tile([P, hi - lo], F32, tag="small", name="y_bank")
+            product(acc[:], w2_codes[:, b * P : (b + 1) * P], w2_scales[:, b * P : (b + 1) * P], h_codes[:, lo:hi], h_scales[:, lo:hi])
+            copy(y_sb[b][:, lo:hi], acc[:])
+
+        def scatter(b, lo, hi):
+            nc.vector.tensor_tensor(windows[b][:].indirect(entries(lo, hi)), y_sb[b][:, lo:hi], gate_picked[:, lo:hi], MULT)
+
+        h0 = first_layer(0)
+        h1 = first_layer(1)
+        quantize_h(0, h0)
+        second_layer(0, 0, 128, nc.vector.tensor_copy)
+        h2 = first_layer(2)
+        quantize_h(1, h1)
+        second_layer(0, 128, 256, nc.scalar.copy)
+        scatter(0, 0, 128)
+        h3 = first_layer(3)
+        quantize_h(2, h2)
+        scatter(0, 128, 256)
+        quantize_h(3, h3)
+        second_layer(1, 0, 256, nc.scalar.copy)
+        second_layer(0, 256, 512, nc.scalar.copy)
+        second_layer(1, 256, 512, nc.scalar.copy)
+        scatter(1, 0, 256)
+        scatter(0, 256, 512)
+        nc.sync.dma_start(out=out[0:P, :], in_=windows[0][:])
+        scatter(1, 256, 512)
+        nc.sync.dma_start(out=out[P : 2 * P, :], in_=windows[1][:])

@@ -19,6 +19,7 @@ P = 128
 PACK = 4
 CHUNK = 128
 LIST_COLS = 16
+HALF = P // 2
 
 
 def tile_picked_modgate_mlpsilu_l_kernel(tc, xT, gate, w1, w2, offs, out):
@@ -26,7 +27,7 @@ def tile_picked_modgate_mlpsilu_l_kernel(tc, xT, gate, w1, w2, offs, out):
     with ExitStack() as ctx:
         keep = ctx.enter_context(tc.tile_pool(name="keep", bufs=1))
         shared = ctx.enter_context(tc.tile_pool(name="shared", bufs=1))
-        psum = ctx.enter_context(tc.psum_pool(name="psum", bufs=4))
+        psum = ctx.enter_context(tc.psum_pool(name="psum", bufs=1))
 
         def entries(lo, hi):
             return offsets[:, lo // LIST_COLS : hi // LIST_COLS]
@@ -38,51 +39,60 @@ def tile_picked_modgate_mlpsilu_l_kernel(tc, xT, gate, w1, w2, offs, out):
             nc.tensor.matmul_mx(out=acc, lhsT=w_codes.bitcast(FP8X4), lhsT_scale=w_scales,
                                 rhs=a_codes.bitcast(FP8X4), rhs_scale=a_scales, start=True, stop=True)
 
-        gate_row = keep.tile([P, 2, PACK], F32)
-        nc.sync.dma_start(out=gate_row[:], in_=gate[0:1, :].rearrange("o (h p m) -> (o p) h m", h=2, p=P))
+        zero = keep.tile([P, 1], F32)
+        nc.vector.memset(zero[:], 0.0)
+        warm = keep.tile([P, 1], F32)
+        nc.scalar.activation(warm[:], zero[:], ACT.Silu)
+
+        gate_all = keep.tile([P, T], F32)
+        nc.vector.memset(gate_all[:], 0.0)
         x_rows = xT.rearrange("(p j) t -> p j t", j=PACK)
+        w1_rows = w1.rearrange("(p j) c -> p j c", j=PACK)
         x_pieces = [[0,0,512],[0,512,1024],[1,0,512],[1,512,1024]]
         x_raw = []
+        w1_raw = []
         offsets = keep.tile([P, S // LIST_COLS], U16)
-        for i, (u, lo, hi) in enumerate(x_pieces):
-            raw = keep.tile([P, 2, hi - lo], F32, name="x_raw%d" % i, tag="x_raw%d" % i, align_bytes=64)
+
+        def load_x(i):
+            u, lo, hi = x_pieces[i]
+            raw = shared.tile([P, 2, hi - lo], F32, name="x_raw%d" % i, offset=8192 + 4096 * i, align_bytes=64)
             nc.sync.dma_start(out=raw[:], in_=x_rows[:, 2 * u : 2 * u + 2, lo:hi])
             x_raw.append(raw)
-            if i == 0:
-                nc.sync.dma_start(offsets[:], offs)
-        w1_rows = w1.rearrange("(p j) c -> p j c", j=PACK)
-        w1_raw = []
+
+        load_x(0)
+        nc.sync.dma_start(offsets[:], offs)
+        nc.sync.dma_start(out=gate_all[0:1, :], in_=gate[0:1, :])
+        load_x(1)
         for h in range(2):
             raw = keep.tile([P, PACK, H // 2], F32, name="w1_raw%d" % h, tag="w1_raw%d" % h, align_bytes=64)
             nc.sync.dma_start(out=raw[:], in_=w1_rows[:, :, h * (H // 2) : (h + 1) * (H // 2)])
             w1_raw.append(raw)
+        for i in range(2, len(x_pieces)):
+            load_x(i)
         w2_raw = keep.tile([P, PACK, N], F32)
         nc.sync.dma_start(out=w2_raw[:], in_=w2.rearrange("(p j) n -> p j n", j=PACK))
 
         ident = keep.tile([P, P], F32)
         make_identity(nc, ident[:])
-        warm = keep.tile([P, 1], F32)
-        nc.scalar.activation(warm[:], ident[:, 0:1], ACT.Silu)
         windows = [keep.tile([P, T], F32, name="window%d" % b) for b in range(N // P)]
-        for window in windows:
-            nc.vector.memset(window[:], 0.0)
+        nc.vector.memset(windows[0][:], 0.0)
+        nc.gpsimd.memset(windows[1][:], 0.0)
 
-        gate_all = shared.tile([P, T], F32, offset=2048, align_bytes=64)
-        gate_view = gate_all[:].rearrange("q (h p m) -> q h p m", h=2, m=PACK)
-        for half in range(2):
-            bank = psum.tile([P, PACK, P], F32, tag="small", name="gate_bank")
-            for m in range(PACK):
-                nc.tensor.transpose(bank[:, m, :], gate_row[:, half, m : m + 1].to_broadcast([P, P]), ident[:])
-            nc.vector.tensor_copy(gate_view[:, half], bank[:].rearrange("q m p -> q p m"))
+        gate_one = keep.tile([P, S], F32)
+        nc.vector.tensor_copy(gate_one[:], gate_all[:].indirect(offsets[:]))
+        bank = psum.tile([P, PACK, P], F32, tag="bank4", name="gate_bank")
+        for c in range(S // P):
+            nc.tensor.transpose(bank[:, c, :], gate_one[:, c * P : (c + 1) * P], ident[:])
+        gate_cols = keep.tile([P, S // P], F32)
+        nc.scalar.copy(gate_cols[:], bank[:, :, 0])
+        bank = psum.tile([P, PACK, P], F32, tag="bank5", name="gate_bank")
+        for c in range(S // P):
+            nc.tensor.transpose(bank[:, c, :], gate_cols[:, c : c + 1].to_broadcast([P, P]), ident[:])
 
-        gate_picked = keep.tile([P, S], F32)
-        nc.vector.tensor_copy(gate_picked[:], gate_all[:].indirect(offsets[:]))
-
-        x_pairs = [keep.tile([P, T, 2], BF16, name="x_pairs0"), shared.tile([P, T, 2], BF16, name="x_pairs1", offset=0, align_bytes=64)]
-        groups = [[0,128],[128,256],[256,512]]
-        picked = shared.tile([P, S, 2], U32, offset=4096, align_bytes=64)
-        x_codes = [keep.tile([P, CHUNK], U32, align_bytes=64, name="x_codes_first")]
+        picked = keep.tile([P, S, 2], U32, align_bytes=64)
+        x_codes = keep.tile([P, S], U32, align_bytes=64)
         x_scales = keep.tile([P, S], U8, align_bytes=64)
+        x_pairs = []
 
         def cast(i, vector_cols):
             u, lo, hi = x_pieces[i]
@@ -92,62 +102,69 @@ def tile_picked_modgate_mlpsilu_l_kernel(tc, xT, gate, w1, w2, offs, out):
             if vector_cols < hi - lo:
                 nc.scalar.copy(x_pairs[u][:, lo + vector_cols : hi, :], src[:, vector_cols:, :])
 
-        def gather(u):
+        def gather(u, lo, hi):
             window = x_pairs[u][:].rearrange("p t e -> p (t e)").bitcast(U32)
-            nc.vector.tensor_copy(picked[:, :, u], window.indirect(offsets[:]))
+            nc.vector.tensor_copy(picked[:, lo:hi, u], window.indirect(entries(lo, hi)))
 
-        def x_words(lo, hi):
-            return x_codes[0][:, lo:hi] if hi <= CHUNK else x_codes[1][:, lo - CHUNK : hi - CHUNK]
+        def quantize_x(lo, hi):
+            quantize(x_codes[:, lo:hi], x_scales[:, lo:hi], picked[:, lo:hi, :].rearrange("p s u -> p (s u)").bitcast(BF16))
 
-        def quantize_x(g):
-            lo, hi = groups[g]
-            quantize(x_words(lo, hi), x_scales[:, lo:hi], picked[:, lo:hi, :].rearrange("p s u -> p (s u)").bitcast(BF16))
+        shares = [0,256,0,352]
+        x_pairs.append(shared.tile([P, T, 2], BF16, name="x_pairs0", offset=4096, align_bytes=64))
+        cast(0, shares[0])
+        cast(1, shares[1])
+        gather(0, 0, S)
 
-        shares = [0,0,0,320]
-        for i, (u, lo, hi) in enumerate(x_pieces):
-            cast(i, shares[i])
-            if hi == T:
-                gather(u)
-        quantize_x(0)
-
-        half = P // 2
         w1_grouped = [
-            keep.tile([P, PACK, half, PACK], BF16, align_bytes=64, name="w1_grouped0", tag="x_raw3"),
-            shared.tile([P, PACK, half, PACK], BF16, align_bytes=64, name="w1_grouped1", offset=0),
+            keep.tile([P, PACK, HALF, PACK], BF16, align_bytes=64, name="w1_grouped0"),
+            shared.tile([P, PACK, HALF, PACK], BF16, align_bytes=64, name="w1_grouped1", offset=4096),
         ]
-        w1_codes = shared.tile([P, H], U32, align_bytes=64, offset=2048)
+        w1_codes = shared.tile([P, H], U32, align_bytes=64, offset=4096 + 2048)
         w1_scales = keep.tile([P, H], U8, align_bytes=64)
-        for h, copy in enumerate((nc.scalar.copy, nc.vector.tensor_copy)):
-            copy(w1_grouped[h][:].rearrange("p t m j -> p m j t"), w1_raw[h][:].rearrange("p j (m t) -> p m j t", t=PACK))
-        for t in range(PACK):
-            for h in range(2):
-                cols = slice(t * P + h * half, t * P + (h + 1) * half)
+        for h, split in enumerate((0, 40)):
+            dst = w1_grouped[h][:].rearrange("p t m j -> p m j t")
+            src = w1_raw[h][:].rearrange("p j (m t) -> p m j t", t=PACK)
+            if split > 0:
+                nc.vector.tensor_copy(dst[:, :split], src[:, :split])
+            if split < HALF:
+                nc.scalar.copy(dst[:, split:], src[:, split:])
+        for h in range(2):
+            for t in range(PACK):
+                cols = slice(t * P + h * HALF, t * P + (h + 1) * HALF)
                 quantize(w1_codes[:, cols], w1_scales[:, cols], w1_grouped[h][:, t].rearrange("p m j -> p (m j)"))
-        x_codes.append(keep.tile([P, S - CHUNK], U32, align_bytes=64, name="x_codes_rest", tag="w1_raw1"))
-        for g in range(1, len(groups)):
-            quantize_x(g)
+
+        x_pairs.append(keep.tile([P, T, 2], BF16, name="x_pairs1", tag="w1_raw1", align_bytes=64))
+        for i in range(2, len(x_pieces)):
+            cast(i, shares[i])
+        last_x = 8192 + 4096 * (len(x_pieces) - 1)
+        gate_picked = shared.tile([P, S], F32, offset=last_x, align_bytes=64)
+        nc.scalar.copy(gate_picked[:], bank[:].rearrange("q c j -> q (c j)"))
+        gather(1, 128, 256)
+        quantize_x(128, 256)
+        gather(1, 0, 128)
+        quantize_x(0, 128)
+        gather(1, 224, 512)
+        quantize_x(256, 512)
 
         w2_codes = keep.tile([P, N], U32, align_bytes=64)
         w2_scales = keep.tile([P, N], U8, align_bytes=64)
+        w2_grouped = shared.tile([P, N, PACK], BF16, align_bytes=64, offset=last_x + 2048)
         for b in range(N // P):
-            if b == 0:
-                w2_grouped = shared.tile([P, P, PACK], BF16, align_bytes=64, name="w2_grouped0", offset=0)
-            else:
-                w2_grouped = keep.tile([P, P, PACK], BF16, align_bytes=64, name="w2_grouped1", tag="w1_raw0")
-            (nc.vector.tensor_copy, nc.scalar.copy)[b](w2_grouped[:].rearrange("p (c i) j -> p c j i", i=4),
-                w2_raw[:, :, b * P : (b + 1) * P].rearrange("p j (c i) -> p c j i", i=4))
-            quantize(w2_codes[:, b * P : (b + 1) * P], w2_scales[:, b * P : (b + 1) * P], w2_grouped[:].rearrange("p n j -> p (n j)"))
+            nc.scalar.copy(w2_grouped[:, b * P : (b + 1) * P, :].rearrange("p (c i) j -> p c j i", i=4),
+                           w2_raw[:, :, b * P : (b + 1) * P].rearrange("p j (c i) -> p c j i", i=4))
 
+        def quantize_w2(b):
+            quantize(w2_codes[:, b * P : (b + 1) * P], w2_scales[:, b * P : (b + 1) * P], w2_grouped[:, b * P : (b + 1) * P, :].rearrange("p n j -> p (n j)"))
 
         y_sb = [keep.tile([P, S], F32, name="y_sb%d" % b) for b in range(N // P)]
         h_codes = keep.tile([P, S], U32, align_bytes=64)
         h_scales = keep.tile([P, S], U8, align_bytes=64)
 
-        def first_layer(c):
+        def first_layer(c, tag):
             cols = slice(c * CHUNK, (c + 1) * CHUNK)
-            bank = psum.tile([P, PACK, CHUNK], F32, tag="hidden", name="h_bank")
+            bank = psum.tile([P, PACK, CHUNK], F32, tag=tag, name="h_bank")
             for t in range(PACK):
-                product(bank[:, t, :], w1_codes[:, t * P : (t + 1) * P], w1_scales[:, t * P : (t + 1) * P], x_words(cols.start, cols.stop), x_scales[:, cols])
+                product(bank[:, t, :], w1_codes[:, t * P : (t + 1) * P], w1_scales[:, t * P : (t + 1) * P], x_codes[:, cols], x_scales[:, cols])
             h_grouped = keep.tile([P, CHUNK, PACK], BF16, align_bytes=64, name="h_grouped%d" % c)
             nc.scalar.activation(h_grouped[:], bank[:].rearrange("p t s -> p s t"), ACT.Silu)
             return h_grouped
@@ -156,30 +173,34 @@ def tile_picked_modgate_mlpsilu_l_kernel(tc, xT, gate, w1, w2, offs, out):
             cols = slice(c * CHUNK, (c + 1) * CHUNK)
             quantize(h_codes[:, cols], h_scales[:, cols], h_grouped[:].rearrange("p s t -> p (s t)"))
 
-        def second_layer(b, lo, hi, copy):
-            acc = psum.tile([P, hi - lo], F32, tag="small", name="y_bank")
+        def second_layer(b, lo, hi, copy, tag):
+            acc = psum.tile([P, hi - lo], F32, tag=tag, name="y_bank")
             product(acc[:], w2_codes[:, b * P : (b + 1) * P], w2_scales[:, b * P : (b + 1) * P], h_codes[:, lo:hi], h_scales[:, lo:hi])
             copy(y_sb[b][:, lo:hi], acc[:])
 
         def scatter(b, lo, hi):
             nc.vector.tensor_tensor(windows[b][:].indirect(entries(lo, hi)), y_sb[b][:, lo:hi], gate_picked[:, lo:hi], MULT)
 
-        h0 = first_layer(0)
-        h1 = first_layer(1)
-        quantize_h(0, h0)
-        second_layer(0, 0, 128, nc.vector.tensor_copy)
-        h2 = first_layer(2)
-        quantize_h(1, h1)
-        second_layer(0, 128, 256, nc.scalar.copy)
-        scatter(0, 0, 128)
-        h3 = first_layer(3)
-        quantize_h(2, h2)
+        quantize_w2(0)
+        h_a = first_layer(1, "bank0")
+        h_b = first_layer(0, "bank1")
+        quantize_w2(1)
+        quantize_h(1, h_a)
+        second_layer(0, 128, 256, nc.vector.tensor_copy, "bank2")
+        second_layer(1, 128, 256, nc.scalar.copy, "bank3")
+        quantize_h(0, h_b)
         scatter(0, 128, 256)
-        quantize_h(3, h3)
-        second_layer(1, 0, 256, nc.scalar.copy)
-        second_layer(0, 256, 512, nc.scalar.copy)
-        second_layer(1, 256, 512, nc.scalar.copy)
-        scatter(1, 0, 256)
+        h_c = first_layer(2, "bank2")
+        second_layer(0, 0, 128, nc.scalar.copy, "bank4")
+        scatter(1, 128, 256)
+        quantize_h(2, h_c)
+        h_d = first_layer(3, "bank3")
+        scatter(0, 0, 128)
+        quantize_h(3, h_d)
+        second_layer(1, 0, 128, nc.scalar.copy, "bank5")
+        second_layer(0, 256, 512, nc.scalar.copy, "bank0")
+        second_layer(1, 256, 512, nc.scalar.copy, "bank1")
+        scatter(1, 0, 128)
         scatter(0, 256, 512)
         nc.sync.dma_start(out=out[0:P, :], in_=windows[0][:])
         scatter(1, 256, 512)

@@ -44,31 +44,30 @@ def tile_picked_modgate_mlpsilu_l_kernel(tc, xT, gate, w1, w2, offs, out):
         warm = keep.tile([P, 1], F32)
         nc.scalar.activation(warm[:], zero[:], ACT.Silu)
 
-        gate_all = keep.tile([P, T], F32)
+        gate_all = shared.tile([P, T], F32, offset=0, align_bytes=64)
         nc.vector.memset(gate_all[:], 0.0)
         x_rows = xT.rearrange("(p j) t -> p j t", j=PACK)
         w1_rows = w1.rearrange("(p j) c -> p j c", j=PACK)
-        x_pieces = [[0,0,512],[0,512,1024],[1,0,512],[1,512,1024]]
+        x_pieces = [[0,0,512],[0,512,1024],[1,0,640],[1,640,1024]]
         x_raw = []
         w1_raw = []
         offsets = keep.tile([P, S // LIST_COLS], U16)
 
         def load_x(i):
             u, lo, hi = x_pieces[i]
-            raw = shared.tile([P, 2, hi - lo], F32, name="x_raw%d" % i, offset=8192 + 4096 * i, align_bytes=64)
+            raw = shared.tile([P, 2, hi - lo], F32, name="x_raw%d" % i, offset=16384 + 8192 * i, align_bytes=64)
             nc.sync.dma_start(out=raw[:], in_=x_rows[:, 2 * u : 2 * u + 2, lo:hi])
             x_raw.append(raw)
 
         load_x(0)
         nc.sync.dma_start(offsets[:], offs)
         nc.sync.dma_start(out=gate_all[0:1, :], in_=gate[0:1, :])
-        load_x(1)
+        for i in range(1, len(x_pieces)):
+            load_x(i)
         for h in range(2):
-            raw = keep.tile([P, PACK, H // 2], F32, name="w1_raw%d" % h, tag="w1_raw%d" % h, align_bytes=64)
+            raw = shared.tile([P, PACK, H // 2], F32, name="w1_raw%d" % h, offset=4096 + 4096 * h, align_bytes=64)
             nc.sync.dma_start(out=raw[:], in_=w1_rows[:, :, h * (H // 2) : (h + 1) * (H // 2)])
             w1_raw.append(raw)
-        for i in range(2, len(x_pieces)):
-            load_x(i)
         w2_raw = keep.tile([P, PACK, N], F32)
         nc.sync.dma_start(out=w2_raw[:], in_=w2.rearrange("(p j) n -> p j n", j=PACK))
 
@@ -90,71 +89,60 @@ def tile_picked_modgate_mlpsilu_l_kernel(tc, xT, gate, w1, w2, offs, out):
             nc.tensor.transpose(bank[:, c, :], gate_cols[:, c : c + 1].to_broadcast([P, P]), ident[:])
 
         picked = keep.tile([P, S, 2], U32, align_bytes=64)
-        x_codes = keep.tile([P, S], U32, align_bytes=64)
         x_scales = keep.tile([P, S], U8, align_bytes=64)
-        x_pairs = []
-
-        def cast(i, vector_cols):
-            u, lo, hi = x_pieces[i]
+        x_pairs = [keep.tile([P, T, 2], BF16, name="x_pairs0"), shared.tile([P, T, 2], BF16, name="x_pairs1", offset=0, align_bytes=64)]
+        shares = [0,256,320,0]
+        for i, (u, lo, hi) in enumerate(x_pieces):
             src = x_raw[i][:].rearrange("p e t -> p t e")
-            if vector_cols > 0:
-                nc.vector.tensor_copy(x_pairs[u][:, lo : lo + vector_cols, :], src[:, :vector_cols, :])
-            if vector_cols < hi - lo:
-                nc.scalar.copy(x_pairs[u][:, lo + vector_cols : hi, :], src[:, vector_cols:, :])
+            split = shares[i]
+            if split > 0:
+                nc.vector.tensor_copy(x_pairs[u][:, lo : lo + split, :], src[:, :split, :])
+            nc.scalar.copy(x_pairs[u][:, lo + split : hi, :], src[:, split:, :])
+            if hi == T:
+                window = x_pairs[u][:].rearrange("p t e -> p (t e)").bitcast(U32)
+                nc.vector.tensor_copy(picked[:, :, u], window.indirect(offsets[:]))
 
-        def gather(u, lo, hi):
-            window = x_pairs[u][:].rearrange("p t e -> p (t e)").bitcast(U32)
-            nc.vector.tensor_copy(picked[:, lo:hi, u], window.indirect(entries(lo, hi)))
+        def quantize_x(codes, lo, hi):
+            quantize(codes, x_scales[:, lo:hi], picked[:, lo:hi, :].rearrange("p s u -> p (s u)").bitcast(BF16))
 
-        def quantize_x(lo, hi):
-            quantize(x_codes[:, lo:hi], x_scales[:, lo:hi], picked[:, lo:hi, :].rearrange("p s u -> p (s u)").bitcast(BF16))
-
-        shares = [0,256,0,352]
-        x_pairs.append(shared.tile([P, T, 2], BF16, name="x_pairs0", offset=4096, align_bytes=64))
-        cast(0, shares[0])
-        cast(1, shares[1])
-        gather(0, 0, S)
+        x_first = keep.tile([P, CHUNK], U32, align_bytes=64)
+        quantize_x(x_first[:], 0, CHUNK)
 
         w1_grouped = [
-            keep.tile([P, PACK, HALF, PACK], BF16, align_bytes=64, name="w1_grouped0"),
-            shared.tile([P, PACK, HALF, PACK], BF16, align_bytes=64, name="w1_grouped1", offset=4096),
+            shared.tile([P, PACK, HALF, PACK], BF16, align_bytes=64, name="w1_grouped0", offset=16384 + 8192 * 3),
+            shared.tile([P, PACK, HALF, PACK], BF16, align_bytes=64, name="w1_grouped1", offset=0),
         ]
-        w1_codes = shared.tile([P, H], U32, align_bytes=64, offset=4096 + 2048)
+        w1_codes = shared.tile([P, H], U32, align_bytes=64, offset=2048)
         w1_scales = keep.tile([P, H], U8, align_bytes=64)
-        for h, split in enumerate((0, 40)):
+        for h, split in enumerate((0, 32)):
             dst = w1_grouped[h][:].rearrange("p t m j -> p m j t")
             src = w1_raw[h][:].rearrange("p j (m t) -> p m j t", t=PACK)
             if split > 0:
                 nc.vector.tensor_copy(dst[:, :split], src[:, :split])
-            if split < HALF:
-                nc.scalar.copy(dst[:, split:], src[:, split:])
-        for h in range(2):
-            for t in range(PACK):
+            nc.scalar.copy(dst[:, split:], src[:, split:])
+        for t in range(PACK):
+            for h in range(2):
                 cols = slice(t * P + h * HALF, t * P + (h + 1) * HALF)
                 quantize(w1_codes[:, cols], w1_scales[:, cols], w1_grouped[h][:, t].rearrange("p m j -> p (m j)"))
 
-        x_pairs.append(keep.tile([P, T, 2], BF16, name="x_pairs1", tag="w1_raw1", align_bytes=64))
-        for i in range(2, len(x_pieces)):
-            cast(i, shares[i])
-        last_x = 8192 + 4096 * (len(x_pieces) - 1)
-        gate_picked = shared.tile([P, S], F32, offset=last_x, align_bytes=64)
+        gate_picked = shared.tile([P, S], F32, offset=8192, align_bytes=64)
         nc.scalar.copy(gate_picked[:], bank[:].rearrange("q c j -> q (c j)"))
-        gather(1, 128, 256)
-        quantize_x(128, 256)
-        gather(1, 0, 128)
-        quantize_x(0, 128)
-        gather(1, 224, 512)
-        quantize_x(256, 512)
+        x_rest = shared.tile([P, S - CHUNK], U32, offset=8192 + 2048, align_bytes=64)
+        quantize_x(x_rest[:, :CHUNK], CHUNK, 2 * CHUNK)
+        quantize_x(x_rest[:, CHUNK:], 2 * CHUNK, S)
 
         w2_codes = keep.tile([P, N], U32, align_bytes=64)
         w2_scales = keep.tile([P, N], U8, align_bytes=64)
-        w2_grouped = shared.tile([P, N, PACK], BF16, align_bytes=64, offset=last_x + 2048)
-        for b in range(N // P):
-            nc.scalar.copy(w2_grouped[:, b * P : (b + 1) * P, :].rearrange("p (c i) j -> p c j i", i=4),
-                           w2_raw[:, :, b * P : (b + 1) * P].rearrange("p j (c i) -> p c j i", i=4))
+        w2_grouped = [
+            shared.tile([P, P, PACK], BF16, align_bytes=64, name="w2_grouped0", offset=0),
+            shared.tile([P, P, PACK], BF16, align_bytes=64, name="w2_grouped1", offset=8192 + 2048 + 1536),
+        ]
+        for b, copy in enumerate((nc.vector.tensor_copy, nc.scalar.copy)):
+            copy(w2_grouped[b][:].rearrange("p (c i) j -> p c j i", i=4),
+                 w2_raw[:, :, b * P : (b + 1) * P].rearrange("p j (c i) -> p c j i", i=4))
 
         def quantize_w2(b):
-            quantize(w2_codes[:, b * P : (b + 1) * P], w2_scales[:, b * P : (b + 1) * P], w2_grouped[:, b * P : (b + 1) * P, :].rearrange("p n j -> p (n j)"))
+            quantize(w2_codes[:, b * P : (b + 1) * P], w2_scales[:, b * P : (b + 1) * P], w2_grouped[b][:].rearrange("p n j -> p (n j)"))
 
         y_sb = [keep.tile([P, S], F32, name="y_sb%d" % b) for b in range(N // P)]
         h_codes = keep.tile([P, S], U32, align_bytes=64)
@@ -162,9 +150,10 @@ def tile_picked_modgate_mlpsilu_l_kernel(tc, xT, gate, w1, w2, offs, out):
 
         def first_layer(c, tag):
             cols = slice(c * CHUNK, (c + 1) * CHUNK)
+            x_words = x_first[:] if c == 0 else x_rest[:, (c - 1) * CHUNK : c * CHUNK]
             bank = psum.tile([P, PACK, CHUNK], F32, tag=tag, name="h_bank")
             for t in range(PACK):
-                product(bank[:, t, :], w1_codes[:, t * P : (t + 1) * P], w1_scales[:, t * P : (t + 1) * P], x_codes[:, cols], x_scales[:, cols])
+                product(bank[:, t, :], w1_codes[:, t * P : (t + 1) * P], w1_scales[:, t * P : (t + 1) * P], x_words, x_scales[:, cols])
             h_grouped = keep.tile([P, CHUNK, PACK], BF16, align_bytes=64, name="h_grouped%d" % c)
             nc.scalar.activation(h_grouped[:], bank[:].rearrange("p t s -> p s t"), ACT.Silu)
             return h_grouped
@@ -182,25 +171,25 @@ def tile_picked_modgate_mlpsilu_l_kernel(tc, xT, gate, w1, w2, offs, out):
             nc.vector.tensor_tensor(windows[b][:].indirect(entries(lo, hi)), y_sb[b][:, lo:hi], gate_picked[:, lo:hi], MULT)
 
         quantize_w2(0)
-        h_a = first_layer(1, "bank0")
-        h_b = first_layer(0, "bank1")
+        h_a = first_layer(0, "bank0")
+        h_b = first_layer(1, "bank1")
         quantize_w2(1)
-        quantize_h(1, h_a)
-        second_layer(0, 128, 256, nc.vector.tensor_copy, "bank2")
-        second_layer(1, 128, 256, nc.scalar.copy, "bank3")
-        quantize_h(0, h_b)
-        scatter(0, 128, 256)
+        quantize_h(0, h_a)
+        second_layer(0, 0, 128, nc.scalar.copy, "bank2")
+        second_layer(1, 0, 128, nc.scalar.copy, "bank3")
+        quantize_h(1, h_b)
+        scatter(0, 0, 128)
         h_c = first_layer(2, "bank2")
-        second_layer(0, 0, 128, nc.scalar.copy, "bank4")
-        scatter(1, 128, 256)
+        second_layer(0, 128, 256, nc.scalar.copy, "bank4")
+        scatter(1, 0, 128)
         quantize_h(2, h_c)
         h_d = first_layer(3, "bank3")
-        scatter(0, 0, 128)
+        scatter(0, 128, 256)
         quantize_h(3, h_d)
-        second_layer(1, 0, 128, nc.scalar.copy, "bank5")
+        second_layer(1, 128, 256, nc.scalar.copy, "bank5")
         second_layer(0, 256, 512, nc.scalar.copy, "bank0")
         second_layer(1, 256, 512, nc.scalar.copy, "bank1")
-        scatter(1, 0, 128)
+        scatter(1, 128, 256)
         scatter(0, 256, 512)
         nc.sync.dma_start(out=out[0:P, :], in_=windows[0][:])
         scatter(1, 256, 512)

@@ -8,66 +8,76 @@ FLOPS = 2 * S * (K * H + H * N)
 
 F32 = mybir.dt.float32
 BF16 = mybir.dt.bfloat16
+I32 = mybir.dt.int32
 U32 = mybir.dt.uint32
 U16 = mybir.dt.uint16
 U8 = mybir.dt.uint8
 FP8X4 = mybir.dt.float8_e4m3fn_x4
-ACT = mybir.ActivationFunctionType
+SILU = mybir.ActivationFunctionType.Silu
 MULT = mybir.AluOpType.mult
 
 P = 128
 PACK = 4
 CHUNK = 128
-LIST_COLS = 16
-HALF = P // 2
+LIST_COL = 16
+W1_HALF = P // 2
+ALIGN = 64
+
+X_LOADS = ((0, 0, 512, 0), (0, 512, T, 256), (1, 0, 640, 320), (1, 640, T, 0))
+W1_VECTOR_SHARE = 32
+
+FIRST_REGION = 0
+SECOND_REGION = 4 * T
 
 
 def tile_picked_modgate_mlpsilu_l_kernel(tc, xT, gate, w1, w2, offs, out):
     nc = tc.nc
     with ExitStack() as ctx:
         keep = ctx.enter_context(tc.tile_pool(name="keep", bufs=1))
-        shared = ctx.enter_context(tc.tile_pool(name="shared", bufs=1))
+        reuse = ctx.enter_context(tc.tile_pool(name="reuse", bufs=1))
         psum = ctx.enter_context(tc.psum_pool(name="psum", bufs=1))
 
         def entries(lo, hi):
-            return offsets[:, lo // LIST_COLS : hi // LIST_COLS]
+            return offsets[:, lo // LIST_COL : hi // LIST_COL]
 
-        def quantize(codes, scales, values):
-            nc.vector.quantize_mx(out=codes.bitcast(FP8X4), scales=scales, in_=values)
+        def quantize(codes, scales, grouped):
+            nc.vector.quantize_mx(out=codes.bitcast(FP8X4), scales=scales, in_=grouped)
 
         def product(acc, w_codes, w_scales, a_codes, a_scales):
-            nc.tensor.matmul_mx(out=acc, lhsT=w_codes.bitcast(FP8X4), lhsT_scale=w_scales,
-                                rhs=a_codes.bitcast(FP8X4), rhs_scale=a_scales, start=True, stop=True)
+            nc.tensor.matmul_mx(
+                out=acc,
+                lhsT=w_codes.bitcast(FP8X4),
+                lhsT_scale=w_scales,
+                rhs=a_codes.bitcast(FP8X4),
+                rhs_scale=a_scales,
+                start=True,
+                stop=True,
+            )
 
         zero = keep.tile([P, 1], F32)
         nc.vector.memset(zero[:], 0.0)
-        warm = keep.tile([P, 1], F32)
-        nc.scalar.activation(warm[:], zero[:], ACT.Silu)
+        warm_up = keep.tile([P, 1], F32)
+        nc.scalar.activation(warm_up[:], zero[:], SILU)
 
-        gate_all = shared.tile([P, T], F32, offset=0, align_bytes=64)
-        nc.vector.memset(gate_all[:], 0.0)
+        gate_window = reuse.tile([P, T], F32, offset=FIRST_REGION, align_bytes=ALIGN)
+        nc.vector.memset(gate_window[:], 0.0)
+        offsets = keep.tile([P, S // LIST_COL], U16)
         x_rows = xT.rearrange("(p j) t -> p j t", j=PACK)
-        w1_rows = w1.rearrange("(p j) c -> p j c", j=PACK)
-        x_pieces = [[0,0,512],[0,512,1024],[1,0,640],[1,640,1024]]
         x_raw = []
-        w1_raw = []
-        offsets = keep.tile([P, S // LIST_COLS], U16)
-
-        def load_x(i):
-            u, lo, hi = x_pieces[i]
-            raw = shared.tile([P, 2, hi - lo], F32, name="x_raw%d" % i, offset=16384 + 8192 * i, align_bytes=64)
+        for i, (u, lo, hi, vector_tokens) in enumerate(X_LOADS):
+            raw = keep.tile([P, 2, hi - lo], F32, name="x_raw", tag="x_raw%d" % i, align_bytes=ALIGN)
             nc.sync.dma_start(out=raw[:], in_=x_rows[:, 2 * u : 2 * u + 2, lo:hi])
             x_raw.append(raw)
-
-        load_x(0)
-        nc.sync.dma_start(offsets[:], offs)
-        nc.sync.dma_start(out=gate_all[0:1, :], in_=gate[0:1, :])
-        for i in range(1, len(x_pieces)):
-            load_x(i)
-        for h in range(2):
-            raw = shared.tile([P, PACK, H // 2], F32, name="w1_raw%d" % h, offset=4096 + 4096 * h, align_bytes=64)
-            nc.sync.dma_start(out=raw[:], in_=w1_rows[:, :, h * (H // 2) : (h + 1) * (H // 2)])
-            w1_raw.append(raw)
+            if i == 0:
+                nc.sync.dma_start(offsets[:], offs)
+                nc.sync.dma_start(out=gate_window[0:1, :], in_=gate[0:1, :])
+        w1_rows = w1.rearrange("(p j) c -> p j c", j=PACK)
+        w1_raw = [
+            keep.tile([P, PACK, H // 2], F32, name="w1_raw0"),
+            reuse.tile([P, PACK, H // 2], F32, name="w1_raw1", offset=SECOND_REGION + 2048, align_bytes=ALIGN),
+        ]
+        for half in range(2):
+            nc.sync.dma_start(out=w1_raw[half][:], in_=w1_rows[:, :, half * (H // 2) : (half + 1) * (H // 2)])
         w2_raw = keep.tile([P, PACK, N], F32)
         nc.sync.dma_start(out=w2_raw[:], in_=w2.rearrange("(p j) n -> p j n", j=PACK))
 
@@ -77,120 +87,126 @@ def tile_picked_modgate_mlpsilu_l_kernel(tc, xT, gate, w1, w2, offs, out):
         nc.vector.memset(windows[0][:], 0.0)
         nc.gpsimd.memset(windows[1][:], 0.0)
 
-        gate_one = keep.tile([P, S], F32)
-        nc.vector.tensor_copy(gate_one[:], gate_all[:].indirect(offsets[:]))
-        bank = psum.tile([P, PACK, P], F32, tag="bank4", name="gate_bank")
+        gate_row = keep.tile([P, S], F32)
+        nc.vector.tensor_copy(gate_row[:], gate_window[:].indirect(offsets[:]))
+        turned = psum.tile([P, S // P, P], F32, tag="bank4")
         for c in range(S // P):
-            nc.tensor.transpose(bank[:, c, :], gate_one[:, c * P : (c + 1) * P], ident[:])
+            nc.tensor.transpose(turned[:, c, :], gate_row[:, c * P : (c + 1) * P], ident[:])
         gate_cols = keep.tile([P, S // P], F32)
-        nc.scalar.copy(gate_cols[:], bank[:, :, 0])
-        bank = psum.tile([P, PACK, P], F32, tag="bank5", name="gate_bank")
+        nc.scalar.copy(gate_cols[:], turned[:, :, 0])
+        spread = psum.tile([P, S // P, P], F32, tag="bank5")
         for c in range(S // P):
-            nc.tensor.transpose(bank[:, c, :], gate_cols[:, c : c + 1].to_broadcast([P, P]), ident[:])
+            nc.tensor.transpose(spread[:, c, :], gate_cols[:, c : c + 1].to_broadcast([P, P]), ident[:])
 
-        picked = keep.tile([P, S, 2], U32, align_bytes=64)
-        x_scales = keep.tile([P, S], U8, align_bytes=64)
-        x_pairs = [keep.tile([P, T, 2], BF16, name="x_pairs0"), shared.tile([P, T, 2], BF16, name="x_pairs1", offset=0, align_bytes=64)]
-        shares = [0,256,320,0]
-        for i, (u, lo, hi) in enumerate(x_pieces):
-            src = x_raw[i][:].rearrange("p e t -> p t e")
-            split = shares[i]
-            if split > 0:
-                nc.vector.tensor_copy(x_pairs[u][:, lo : lo + split, :], src[:, :split, :])
-            nc.scalar.copy(x_pairs[u][:, lo + split : hi, :], src[:, split:, :])
+        picked = keep.tile([P, 2, S], U32)
+        x_pairs = [
+            keep.tile([P, T, 2], BF16, name="x_pairs0"),
+            reuse.tile([P, T, 2], BF16, name="x_pairs1", offset=FIRST_REGION, align_bytes=ALIGN),
+        ]
+        for raw, (u, lo, hi, vector_tokens) in zip(x_raw, X_LOADS):
+            src = raw[:].rearrange("p e t -> p t e")
+            if vector_tokens > 0:
+                nc.vector.tensor_copy(x_pairs[u][:, lo : lo + vector_tokens, :], src[:, :vector_tokens, :])
+            nc.scalar.copy(x_pairs[u][:, lo + vector_tokens : hi, :], src[:, vector_tokens:, :])
             if hi == T:
-                window = x_pairs[u][:].rearrange("p t e -> p (t e)").bitcast(U32)
-                nc.vector.tensor_copy(picked[:, :, u], window.indirect(offsets[:]))
+                pair_words = x_pairs[u][:].rearrange("p t e -> p (t e)").bitcast(U32)
+                nc.vector.tensor_copy(picked[:, u, :], pair_words.indirect(offsets[:]))
 
-        def quantize_x(codes, lo, hi):
-            quantize(codes, x_scales[:, lo:hi], picked[:, lo:hi, :].rearrange("p s u -> p (s u)").bitcast(BF16))
+        picked_words = picked[:].bitcast(I32).rearrange("p u s -> p s u")
+        x_codes = keep.tile([P, S], U32, align_bytes=ALIGN)
+        x_scales = keep.tile([P, S], U8, align_bytes=ALIGN)
 
-        x_first = keep.tile([P, CHUNK], U32, align_bytes=64)
-        quantize_x(x_first[:], 0, CHUNK)
+        def quantize_x(lo, hi, grouped_words):
+            quantize(x_codes[:, lo:hi], x_scales[:, lo:hi], grouped_words.rearrange("p s u -> p (s u)").bitcast(BF16))
+
+        x_first = keep.tile([P, CHUNK, 2], I32, align_bytes=ALIGN)
+        nc.vector.tensor_copy(x_first[:], picked_words[:, :CHUNK, :])
+        quantize_x(0, CHUNK, x_first[:])
 
         w1_grouped = [
-            shared.tile([P, PACK, HALF, PACK], BF16, align_bytes=64, name="w1_grouped0", offset=16384 + 8192 * 3),
-            shared.tile([P, PACK, HALF, PACK], BF16, align_bytes=64, name="w1_grouped1", offset=0),
+            keep.tile([P, PACK, W1_HALF, PACK], BF16, name="w1_grouped0", tag="x_raw3", align_bytes=ALIGN),
+            reuse.tile([P, PACK, W1_HALF, PACK], BF16, name="w1_grouped1", offset=FIRST_REGION, align_bytes=ALIGN),
         ]
-        w1_codes = shared.tile([P, H], U32, align_bytes=64, offset=2048)
-        w1_scales = keep.tile([P, H], U8, align_bytes=64)
-        for h, split in enumerate((0, 32)):
-            dst = w1_grouped[h][:].rearrange("p t m j -> p m j t")
-            src = w1_raw[h][:].rearrange("p j (m t) -> p m j t", t=PACK)
-            if split > 0:
-                nc.vector.tensor_copy(dst[:, :split], src[:, :split])
-            nc.scalar.copy(dst[:, split:], src[:, split:])
+        w1_codes = reuse.tile([P, H], U32, offset=FIRST_REGION + 2048, align_bytes=ALIGN)
+        w1_scales = keep.tile([P, H], U8, align_bytes=ALIGN)
+        for half, vector_groups in enumerate((0, W1_VECTOR_SHARE)):
+            dst = w1_grouped[half][:].rearrange("p t m j -> p m t j")
+            src = w1_raw[half][:].rearrange("p j (m t) -> p m t j", t=PACK)
+            if vector_groups > 0:
+                nc.vector.tensor_copy(dst[:, :vector_groups], src[:, :vector_groups])
+            nc.scalar.copy(dst[:, vector_groups:], src[:, vector_groups:])
         for t in range(PACK):
-            for h in range(2):
-                cols = slice(t * P + h * HALF, t * P + (h + 1) * HALF)
-                quantize(w1_codes[:, cols], w1_scales[:, cols], w1_grouped[h][:, t].rearrange("p m j -> p (m j)"))
+            for half in range(2):
+                cols = slice(t * P + half * W1_HALF, t * P + (half + 1) * W1_HALF)
+                quantize(w1_codes[:, cols], w1_scales[:, cols], w1_grouped[half][:, t].rearrange("p m j -> p (m j)"))
 
-        gate_picked = shared.tile([P, S], F32, offset=8192, align_bytes=64)
-        nc.scalar.copy(gate_picked[:], bank[:].rearrange("q c j -> q (c j)"))
-        x_rest = shared.tile([P, S - CHUNK], U32, offset=8192 + 2048, align_bytes=64)
-        quantize_x(x_rest[:, :CHUNK], CHUNK, 2 * CHUNK)
-        quantize_x(x_rest[:, CHUNK:], 2 * CHUNK, S)
+        gate_picked = reuse.tile([P, S], F32, offset=SECOND_REGION + 3072, align_bytes=ALIGN)
+        nc.scalar.copy(gate_picked[:], spread[:].rearrange("q c j -> q (c j)"))
+        x_rest = reuse.tile([P, S - CHUNK, 2], I32, offset=SECOND_REGION, align_bytes=ALIGN)
+        nc.vector.tensor_copy(x_rest[:], picked_words[:, CHUNK:, :])
+        quantize_x(CHUNK, 2 * CHUNK, x_rest[:, :CHUNK, :])
+        quantize_x(2 * CHUNK, S, x_rest[:, CHUNK:, :])
 
-        w2_codes = keep.tile([P, N], U32, align_bytes=64)
-        w2_scales = keep.tile([P, N], U8, align_bytes=64)
+        w2_codes = keep.tile([P, N], U32, align_bytes=ALIGN)
+        w2_scales = keep.tile([P, N], U8, align_bytes=ALIGN)
         w2_grouped = [
-            shared.tile([P, P, PACK], BF16, align_bytes=64, name="w2_grouped0", offset=0),
-            shared.tile([P, P, PACK], BF16, align_bytes=64, name="w2_grouped1", offset=8192 + 2048 + 1536),
+            reuse.tile([P, P, PACK], BF16, name="w2_grouped0", offset=FIRST_REGION, align_bytes=ALIGN),
+            reuse.tile([P, P, PACK], BF16, name="w2_grouped1", offset=SECOND_REGION + 5120, align_bytes=ALIGN),
         ]
         for b, copy in enumerate((nc.vector.tensor_copy, nc.scalar.copy)):
-            copy(w2_grouped[b][:].rearrange("p (c i) j -> p c j i", i=4),
-                 w2_raw[:, :, b * P : (b + 1) * P].rearrange("p j (c i) -> p c j i", i=4))
+            copy(w2_grouped[b][:], w2_raw[:, :, b * P : (b + 1) * P].rearrange("p j n -> p n j"))
 
         def quantize_w2(b):
-            quantize(w2_codes[:, b * P : (b + 1) * P], w2_scales[:, b * P : (b + 1) * P], w2_grouped[b][:].rearrange("p n j -> p (n j)"))
+            cols = slice(b * P, (b + 1) * P)
+            quantize(w2_codes[:, cols], w2_scales[:, cols], w2_grouped[b][:].rearrange("p n j -> p (n j)"))
 
-        y_sb = [keep.tile([P, S], F32, name="y_sb%d" % b) for b in range(N // P)]
-        h_codes = keep.tile([P, S], U32, align_bytes=64)
-        h_scales = keep.tile([P, S], U8, align_bytes=64)
+        y_rows = [keep.tile([P, S], F32, name="y_rows%d" % b) for b in range(N // P)]
+        h_grouped = [keep.tile([P, CHUNK, PACK], BF16, name="h_grouped%d" % c, align_bytes=ALIGN) for c in range(S // CHUNK)]
+        h_codes = keep.tile([P, S], U32, align_bytes=ALIGN)
+        h_scales = keep.tile([P, S], U8, align_bytes=ALIGN)
 
-        def first_layer(c, tag):
+        def first_layer(c, bank):
             cols = slice(c * CHUNK, (c + 1) * CHUNK)
-            x_words = x_first[:] if c == 0 else x_rest[:, (c - 1) * CHUNK : c * CHUNK]
-            bank = psum.tile([P, PACK, CHUNK], F32, tag=tag, name="h_bank")
+            hidden = psum.tile([P, PACK, CHUNK], F32, tag=bank)
             for t in range(PACK):
-                product(bank[:, t, :], w1_codes[:, t * P : (t + 1) * P], w1_scales[:, t * P : (t + 1) * P], x_words, x_scales[:, cols])
-            h_grouped = keep.tile([P, CHUNK, PACK], BF16, align_bytes=64, name="h_grouped%d" % c)
-            nc.scalar.activation(h_grouped[:], bank[:].rearrange("p t s -> p s t"), ACT.Silu)
-            return h_grouped
+                units = slice(t * P, (t + 1) * P)
+                product(hidden[:, t, :], w1_codes[:, units], w1_scales[:, units], x_codes[:, cols], x_scales[:, cols])
+            nc.scalar.activation(h_grouped[c][:], hidden[:].rearrange("p t s -> p s t"), SILU)
 
-        def quantize_h(c, h_grouped):
+        def quantize_h(c):
             cols = slice(c * CHUNK, (c + 1) * CHUNK)
-            quantize(h_codes[:, cols], h_scales[:, cols], h_grouped[:].rearrange("p s t -> p (s t)"))
+            quantize(h_codes[:, cols], h_scales[:, cols], h_grouped[c][:].rearrange("p s t -> p (s t)"))
 
-        def second_layer(b, lo, hi, copy, tag):
-            acc = psum.tile([P, hi - lo], F32, tag=tag, name="y_bank")
-            product(acc[:], w2_codes[:, b * P : (b + 1) * P], w2_scales[:, b * P : (b + 1) * P], h_codes[:, lo:hi], h_scales[:, lo:hi])
-            copy(y_sb[b][:, lo:hi], acc[:])
+        def second_layer(b, lo, hi, bank):
+            rows = slice(b * P, (b + 1) * P)
+            acc = psum.tile([P, hi - lo], F32, tag=bank)
+            product(acc[:], w2_codes[:, rows], w2_scales[:, rows], h_codes[:, lo:hi], h_scales[:, lo:hi])
+            nc.scalar.copy(y_rows[b][:, lo:hi], acc[:])
 
         def scatter(b, lo, hi):
-            nc.vector.tensor_tensor(windows[b][:].indirect(entries(lo, hi)), y_sb[b][:, lo:hi], gate_picked[:, lo:hi], MULT)
+            nc.vector.tensor_tensor(windows[b][:].indirect(entries(lo, hi)), y_rows[b][:, lo:hi], gate_picked[:, lo:hi], MULT)
 
         quantize_w2(0)
-        h_a = first_layer(0, "bank0")
-        h_b = first_layer(1, "bank1")
+        first_layer(0, "bank0")
+        first_layer(1, "bank1")
         quantize_w2(1)
-        quantize_h(0, h_a)
-        second_layer(0, 0, 128, nc.scalar.copy, "bank2")
-        second_layer(1, 0, 128, nc.scalar.copy, "bank3")
-        quantize_h(1, h_b)
-        scatter(0, 0, 128)
-        h_c = first_layer(2, "bank2")
-        second_layer(0, 128, 256, nc.scalar.copy, "bank4")
-        scatter(1, 0, 128)
-        quantize_h(2, h_c)
-        h_d = first_layer(3, "bank3")
-        scatter(0, 128, 256)
-        quantize_h(3, h_d)
-        second_layer(1, 128, 256, nc.scalar.copy, "bank5")
-        second_layer(0, 256, 512, nc.scalar.copy, "bank0")
-        second_layer(1, 256, 512, nc.scalar.copy, "bank1")
-        scatter(1, 128, 256)
-        scatter(0, 256, 512)
+        quantize_h(0)
+        second_layer(0, 0, CHUNK, "bank2")
+        second_layer(1, 0, CHUNK, "bank3")
+        quantize_h(1)
+        scatter(0, 0, CHUNK)
+        first_layer(2, "bank2")
+        second_layer(0, CHUNK, 2 * CHUNK, "bank4")
+        scatter(1, 0, CHUNK)
+        quantize_h(2)
+        first_layer(3, "bank3")
+        scatter(0, CHUNK, 2 * CHUNK)
+        quantize_h(3)
+        second_layer(1, CHUNK, 2 * CHUNK, "bank5")
+        second_layer(0, 2 * CHUNK, S, "bank0")
+        second_layer(1, 2 * CHUNK, S, "bank1")
+        scatter(1, CHUNK, 2 * CHUNK)
+        scatter(0, 2 * CHUNK, S)
         nc.sync.dma_start(out=out[0:P, :], in_=windows[0][:])
-        scatter(1, 256, 512)
+        scatter(1, 2 * CHUNK, S)
         nc.sync.dma_start(out=out[P : 2 * P, :], in_=windows[1][:])

@@ -8,7 +8,6 @@ FLOPS = 2 * S * (K * H + H * N)
 
 F32 = mybir.dt.float32
 BF16 = mybir.dt.bfloat16
-I32 = mybir.dt.int32
 U32 = mybir.dt.uint32
 U16 = mybir.dt.uint16
 U8 = mybir.dt.uint8
@@ -23,7 +22,7 @@ LIST_COL = 16
 W1_HALF = P // 2
 ALIGN = 64
 
-X_LOADS = ((0, 0, 512, 0), (0, 512, T, 256), (1, 0, 640, 320), (1, 640, T, 0))
+X_LOADS = ((0, 0, 384, 0), (0, 384, 768, 0), (0, 768, T, 0), (1, 0, 640, 320), (1, 640, T, 0))
 W1_VECTOR_SHARE = 32
 
 FIRST_REGION = 0
@@ -54,7 +53,7 @@ def tile_picked_modgate_mlpsilu_l_kernel(tc, xT, gate, w1, w2, offs, out):
                 stop=True,
             )
 
-        zero = keep.tile([P, 1], F32)
+        zero = keep.tile([P, 1], F32, tag="zero_then_ident")
         nc.vector.memset(zero[:], 0.0)
         warm_up = keep.tile([P, 1], F32)
         nc.scalar.activation(warm_up[:], zero[:], SILU)
@@ -68,24 +67,24 @@ def tile_picked_modgate_mlpsilu_l_kernel(tc, xT, gate, w1, w2, offs, out):
             raw = keep.tile([P, 2, hi - lo], F32, name="x_raw", tag="x_raw%d" % i, align_bytes=ALIGN)
             nc.sync.dma_start(out=raw[:], in_=x_rows[:, 2 * u : 2 * u + 2, lo:hi])
             x_raw.append(raw)
-            if i == 0:
+            if i == 1:
                 nc.sync.dma_start(offsets[:], offs)
                 nc.sync.dma_start(out=gate_window[0:1, :], in_=gate[0:1, :])
         w1_rows = w1.rearrange("(p j) c -> p j c", j=PACK)
         w1_raw = [
             keep.tile([P, PACK, H // 2], F32, name="w1_raw0"),
-            reuse.tile([P, PACK, H // 2], F32, name="w1_raw1", offset=SECOND_REGION + 2048, align_bytes=ALIGN),
+            reuse.tile([P, PACK, H // 2], F32, name="w1_raw1", offset=SECOND_REGION, align_bytes=ALIGN),
         ]
         for half in range(2):
             nc.sync.dma_start(out=w1_raw[half][:], in_=w1_rows[:, :, half * (H // 2) : (half + 1) * (H // 2)])
         w2_raw = keep.tile([P, PACK, N], F32)
         nc.sync.dma_start(out=w2_raw[:], in_=w2.rearrange("(p j) n -> p j n", j=PACK))
 
-        ident = keep.tile([P, P], F32)
+        ident = keep.tile([P, P], F32, tag="zero_then_ident")
         make_identity(nc, ident[:])
         windows = [keep.tile([P, T], F32, name="window%d" % b) for b in range(N // P)]
-        nc.vector.memset(windows[0][:], 0.0)
-        nc.gpsimd.memset(windows[1][:], 0.0)
+        for window in windows:
+            nc.vector.memset(window[:], 0.0)
 
         gate_row = keep.tile([P, S], F32)
         nc.vector.tensor_copy(gate_row[:], gate_window[:].indirect(offsets[:]))
@@ -98,7 +97,7 @@ def tile_picked_modgate_mlpsilu_l_kernel(tc, xT, gate, w1, w2, offs, out):
         for c in range(S // P):
             nc.tensor.transpose(spread[:, c, :], gate_cols[:, c : c + 1].to_broadcast([P, P]), ident[:])
 
-        picked = keep.tile([P, 2, S], U32)
+        picked = keep.tile([P, S, 2], U32, align_bytes=ALIGN)
         x_pairs = [
             keep.tile([P, T, 2], BF16, name="x_pairs0"),
             reuse.tile([P, T, 2], BF16, name="x_pairs1", offset=FIRST_REGION, align_bytes=ALIGN),
@@ -110,28 +109,25 @@ def tile_picked_modgate_mlpsilu_l_kernel(tc, xT, gate, w1, w2, offs, out):
             nc.scalar.copy(x_pairs[u][:, lo + vector_tokens : hi, :], src[:, vector_tokens:, :])
             if hi == T:
                 pair_words = x_pairs[u][:].rearrange("p t e -> p (t e)").bitcast(U32)
-                nc.vector.tensor_copy(picked[:, u, :], pair_words.indirect(offsets[:]))
+                nc.vector.tensor_copy(picked[:, :, u], pair_words.indirect(offsets[:]))
 
-        picked_words = picked[:].bitcast(I32).rearrange("p u s -> p s u")
-        x_codes = keep.tile([P, S], U32, align_bytes=ALIGN)
         x_scales = keep.tile([P, S], U8, align_bytes=ALIGN)
 
-        def quantize_x(lo, hi, grouped_words):
-            quantize(x_codes[:, lo:hi], x_scales[:, lo:hi], grouped_words.rearrange("p s u -> p (s u)").bitcast(BF16))
+        def quantize_x(codes, lo, hi):
+            quantize(codes, x_scales[:, lo:hi], picked[:, lo:hi, :].rearrange("p s u -> p (s u)").bitcast(BF16))
 
-        x_first = keep.tile([P, CHUNK, 2], I32, align_bytes=ALIGN)
-        nc.vector.tensor_copy(x_first[:], picked_words[:, :CHUNK, :])
-        quantize_x(0, CHUNK, x_first[:])
+        x_codes_first = keep.tile([P, CHUNK], U32, align_bytes=ALIGN)
+        quantize_x(x_codes_first[:], 0, CHUNK)
 
         w1_grouped = [
-            keep.tile([P, PACK, W1_HALF, PACK], BF16, name="w1_grouped0", tag="x_raw3", align_bytes=ALIGN),
+            keep.tile([P, PACK, W1_HALF, PACK], BF16, name="w1_grouped0", tag="x_raw%d" % (len(X_LOADS) - 1), align_bytes=ALIGN),
             reuse.tile([P, PACK, W1_HALF, PACK], BF16, name="w1_grouped1", offset=FIRST_REGION, align_bytes=ALIGN),
         ]
         w1_codes = reuse.tile([P, H], U32, offset=FIRST_REGION + 2048, align_bytes=ALIGN)
         w1_scales = keep.tile([P, H], U8, align_bytes=ALIGN)
         for half, vector_groups in enumerate((0, W1_VECTOR_SHARE)):
-            dst = w1_grouped[half][:].rearrange("p t m j -> p m t j")
-            src = w1_raw[half][:].rearrange("p j (m t) -> p m t j", t=PACK)
+            dst = w1_grouped[half][:].rearrange("p t m j -> p m j t")
+            src = w1_raw[half][:].rearrange("p j (m t) -> p m j t", t=PACK)
             if vector_groups > 0:
                 nc.vector.tensor_copy(dst[:, :vector_groups], src[:, :vector_groups])
             nc.scalar.copy(dst[:, vector_groups:], src[:, vector_groups:])
@@ -140,21 +136,23 @@ def tile_picked_modgate_mlpsilu_l_kernel(tc, xT, gate, w1, w2, offs, out):
                 cols = slice(t * P + half * W1_HALF, t * P + (half + 1) * W1_HALF)
                 quantize(w1_codes[:, cols], w1_scales[:, cols], w1_grouped[half][:, t].rearrange("p m j -> p (m j)"))
 
-        gate_picked = reuse.tile([P, S], F32, offset=SECOND_REGION + 3072, align_bytes=ALIGN)
+        gate_picked = reuse.tile([P, S], F32, offset=SECOND_REGION, align_bytes=ALIGN)
         nc.scalar.copy(gate_picked[:], spread[:].rearrange("q c j -> q (c j)"))
-        x_rest = reuse.tile([P, S - CHUNK, 2], I32, offset=SECOND_REGION, align_bytes=ALIGN)
-        nc.vector.tensor_copy(x_rest[:], picked_words[:, CHUNK:, :])
-        quantize_x(CHUNK, 2 * CHUNK, x_rest[:, :CHUNK, :])
-        quantize_x(2 * CHUNK, S, x_rest[:, CHUNK:, :])
+        x_codes_rest = reuse.tile([P, S - CHUNK], U32, offset=SECOND_REGION + 2048, align_bytes=ALIGN)
+        quantize_x(x_codes_rest[:, :CHUNK], CHUNK, 2 * CHUNK)
+        quantize_x(x_codes_rest[:, CHUNK:], 2 * CHUNK, S)
 
         w2_codes = keep.tile([P, N], U32, align_bytes=ALIGN)
         w2_scales = keep.tile([P, N], U8, align_bytes=ALIGN)
         w2_grouped = [
             reuse.tile([P, P, PACK], BF16, name="w2_grouped0", offset=FIRST_REGION, align_bytes=ALIGN),
-            reuse.tile([P, P, PACK], BF16, name="w2_grouped1", offset=SECOND_REGION + 5120, align_bytes=ALIGN),
+            reuse.tile([P, P, PACK], BF16, name="w2_grouped1", offset=SECOND_REGION + 3584, align_bytes=ALIGN),
         ]
         for b, copy in enumerate((nc.vector.tensor_copy, nc.scalar.copy)):
-            copy(w2_grouped[b][:], w2_raw[:, :, b * P : (b + 1) * P].rearrange("p j n -> p n j"))
+            copy(
+                w2_grouped[b][:].rearrange("p (c i) j -> p c j i", i=PACK),
+                w2_raw[:, :, b * P : (b + 1) * P].rearrange("p j (c i) -> p c j i", i=PACK),
+            )
 
         def quantize_w2(b):
             cols = slice(b * P, (b + 1) * P)
@@ -167,10 +165,11 @@ def tile_picked_modgate_mlpsilu_l_kernel(tc, xT, gate, w1, w2, offs, out):
 
         def first_layer(c, bank):
             cols = slice(c * CHUNK, (c + 1) * CHUNK)
+            x_codes = x_codes_first[:] if c == 0 else x_codes_rest[:, (c - 1) * CHUNK : c * CHUNK]
             hidden = psum.tile([P, PACK, CHUNK], F32, tag=bank)
             for t in range(PACK):
                 units = slice(t * P, (t + 1) * P)
-                product(hidden[:, t, :], w1_codes[:, units], w1_scales[:, units], x_codes[:, cols], x_scales[:, cols])
+                product(hidden[:, t, :], w1_codes[:, units], w1_scales[:, units], x_codes, x_scales[:, cols])
             nc.scalar.activation(h_grouped[c][:], hidden[:].rearrange("p t s -> p s t"), SILU)
 
         def quantize_h(c):

from contextlib import ExitStack

import concourse.mybir as mybir
from concourse.masks import make_identity

K, T, S, H, N = 512, 1024, 512, 512, 256
FLOPS = 2 * S * (K * H + H * N)

F32 = mybir.dt.float32
BF16 = mybir.dt.bfloat16
U32 = mybir.dt.uint32
U16 = mybir.dt.uint16
U8 = mybir.dt.uint8
FP8X4 = mybir.dt.float8_e4m3fn_x4
SILU = mybir.ActivationFunctionType.Silu
MULT = mybir.AluOpType.mult

P = 128
PACK = 4
CHUNK = 128
LIST_COL = 16
W1_HALF = P // 2
ALIGN = 64

X_LOADS = ((0, 0, 384, 0), (0, 384, 768, 0), (0, 768, T, 0), (1, 0, 640, 320), (1, 640, T, 0))
W1_VECTOR_SHARE = 32

FIRST_REGION = 0
SECOND_REGION = 4 * T


def tile_picked_modgate_mlpsilu_l_kernel(tc, xT, gate, w1, w2, offs, out):
    nc = tc.nc
    with ExitStack() as ctx:
        keep = ctx.enter_context(tc.tile_pool(name="keep", bufs=1))
        reuse = ctx.enter_context(tc.tile_pool(name="reuse", bufs=1))
        psum = ctx.enter_context(tc.psum_pool(name="psum", bufs=1))

        def entries(lo, hi):
            return offsets[:, lo // LIST_COL : hi // LIST_COL]

        def quantize(codes, scales, grouped):
            nc.vector.quantize_mx(out=codes.bitcast(FP8X4), scales=scales, in_=grouped)

        def product(acc, w_codes, w_scales, a_codes, a_scales):
            nc.tensor.matmul_mx(
                out=acc,
                lhsT=w_codes.bitcast(FP8X4),
                lhsT_scale=w_scales,
                rhs=a_codes.bitcast(FP8X4),
                rhs_scale=a_scales,
                start=True,
                stop=True,
            )

        zero = keep.tile([P, 1], F32, tag="zero_then_ident")
        nc.vector.memset(zero[:], 0.0)
        warm_up = keep.tile([P, 1], F32)
        nc.scalar.activation(warm_up[:], zero[:], SILU)

        gate_window = reuse.tile([P, T], F32, offset=FIRST_REGION, align_bytes=ALIGN)
        nc.vector.memset(gate_window[:], 0.0)
        offsets = keep.tile([P, S // LIST_COL], U16)
        x_rows = xT.rearrange("(p j) t -> p j t", j=PACK)
        x_raw = []
        for i, (u, lo, hi, vector_tokens) in enumerate(X_LOADS):
            raw = keep.tile([P, 2, hi - lo], F32, name="x_raw", tag="x_raw%d" % i, align_bytes=ALIGN)
            nc.sync.dma_start(out=raw[:], in_=x_rows[:, 2 * u : 2 * u + 2, lo:hi])
            x_raw.append(raw)
            if i == 1:
                nc.sync.dma_start(offsets[:], offs)
                nc.sync.dma_start(out=gate_window[0:1, :], in_=gate[0:1, :])
        w1_rows = w1.rearrange("(p j) c -> p j c", j=PACK)
        w1_raw = [
            keep.tile([P, PACK, H // 2], F32, name="w1_raw0"),
            reuse.tile([P, PACK, H // 2], F32, name="w1_raw1", offset=SECOND_REGION, align_bytes=ALIGN),
        ]
        for half in range(2):
            nc.sync.dma_start(out=w1_raw[half][:], in_=w1_rows[:, :, half * (H // 2) : (half + 1) * (H // 2)])
        w2_raw = keep.tile([P, PACK, N], F32)
        nc.sync.dma_start(out=w2_raw[:], in_=w2.rearrange("(p j) n -> p j n", j=PACK))

        ident = keep.tile([P, P], F32, tag="zero_then_ident")
        make_identity(nc, ident[:])
        windows = [keep.tile([P, T], F32, name="window%d" % b) for b in range(N // P)]
        for window in windows:
            nc.vector.memset(window[:], 0.0)

        gate_row = keep.tile([P, S], F32)
        nc.vector.tensor_copy(gate_row[:], gate_window[:].indirect(offsets[:]))
        turned = psum.tile([P, S // P, P], F32, tag="bank4")
        for c in range(S // P):
            nc.tensor.transpose(turned[:, c, :], gate_row[:, c * P : (c + 1) * P], ident[:])
        gate_cols = keep.tile([P, S // P], F32)
        nc.scalar.copy(gate_cols[:], turned[:, :, 0])
        spread = psum.tile([P, S // P, P], F32, tag="bank5")
        for c in range(S // P):
            nc.tensor.transpose(spread[:, c, :], gate_cols[:, c : c + 1].to_broadcast([P, P]), ident[:])

        picked = keep.tile([P, S, 2], U32, align_bytes=ALIGN)
        x_pairs = [
            keep.tile([P, T, 2], BF16, name="x_pairs0"),
            reuse.tile([P, T, 2], BF16, name="x_pairs1", offset=FIRST_REGION, align_bytes=ALIGN),
        ]
        for raw, (u, lo, hi, vector_tokens) in zip(x_raw, X_LOADS):
            src = raw[:].rearrange("p e t -> p t e")
            if vector_tokens > 0:
                nc.vector.tensor_copy(x_pairs[u][:, lo : lo + vector_tokens, :], src[:, :vector_tokens, :])
            nc.scalar.copy(x_pairs[u][:, lo + vector_tokens : hi, :], src[:, vector_tokens:, :])
            if hi == T:
                pair_words = x_pairs[u][:].rearrange("p t e -> p (t e)").bitcast(U32)
                nc.vector.tensor_copy(picked[:, :, u], pair_words.indirect(offsets[:]))

        x_scales = keep.tile([P, S], U8, align_bytes=ALIGN)

        def quantize_x(codes, lo, hi):
            quantize(codes, x_scales[:, lo:hi], picked[:, lo:hi, :].rearrange("p s u -> p (s u)").bitcast(BF16))

        x_codes_first = keep.tile([P, CHUNK], U32, align_bytes=ALIGN)
        quantize_x(x_codes_first[:], 0, CHUNK)

        w1_grouped = [
            keep.tile([P, PACK, W1_HALF, PACK], BF16, name="w1_grouped0", tag="x_raw%d" % (len(X_LOADS) - 1), align_bytes=ALIGN),
            reuse.tile([P, PACK, W1_HALF, PACK], BF16, name="w1_grouped1", offset=FIRST_REGION, align_bytes=ALIGN),
        ]
        w1_codes = reuse.tile([P, H], U32, offset=FIRST_REGION + 2048, align_bytes=ALIGN)
        w1_scales = keep.tile([P, H], U8, align_bytes=ALIGN)
        for half, vector_groups in enumerate((0, W1_VECTOR_SHARE)):
            dst = w1_grouped[half][:].rearrange("p t m j -> p m j t")
            src = w1_raw[half][:].rearrange("p j (m t) -> p m j t", t=PACK)
            if vector_groups > 0:
                nc.vector.tensor_copy(dst[:, :vector_groups], src[:, :vector_groups])
            nc.scalar.copy(dst[:, vector_groups:], src[:, vector_groups:])
        for t in range(PACK):
            for half in range(2):
                cols = slice(t * P + half * W1_HALF, t * P + (half + 1) * W1_HALF)
                quantize(w1_codes[:, cols], w1_scales[:, cols], w1_grouped[half][:, t].rearrange("p m j -> p (m j)"))

        gate_picked = reuse.tile([P, S], F32, offset=SECOND_REGION, align_bytes=ALIGN)
        nc.scalar.copy(gate_picked[:], spread[:].rearrange("q c j -> q (c j)"))
        x_codes_rest = reuse.tile([P, S - CHUNK], U32, offset=SECOND_REGION + 2048, align_bytes=ALIGN)
        quantize_x(x_codes_rest[:, :CHUNK], CHUNK, 2 * CHUNK)
        quantize_x(x_codes_rest[:, CHUNK:], 2 * CHUNK, S)

        w2_codes = keep.tile([P, N], U32, align_bytes=ALIGN)
        w2_scales = keep.tile([P, N], U8, align_bytes=ALIGN)
        w2_grouped = [
            reuse.tile([P, P, PACK], BF16, name="w2_grouped0", offset=FIRST_REGION, align_bytes=ALIGN),
            reuse.tile([P, P, PACK], BF16, name="w2_grouped1", offset=SECOND_REGION + 3584, align_bytes=ALIGN),
        ]
        for b, copy in enumerate((nc.vector.tensor_copy, nc.scalar.copy)):
            copy(
                w2_grouped[b][:].rearrange("p (c i) j -> p c j i", i=PACK),
                w2_raw[:, :, b * P : (b + 1) * P].rearrange("p j (c i) -> p c j i", i=PACK),
            )

        def quantize_w2(b):
            cols = slice(b * P, (b + 1) * P)
            quantize(w2_codes[:, cols], w2_scales[:, cols], w2_grouped[b][:].rearrange("p n j -> p (n j)"))

        y_rows = [keep.tile([P, S], F32, name="y_rows%d" % b) for b in range(N // P)]
        h_grouped = [keep.tile([P, CHUNK, PACK], BF16, name="h_grouped%d" % c, align_bytes=ALIGN) for c in range(S // CHUNK)]
        h_codes = keep.tile([P, S], U32, align_bytes=ALIGN)
        h_scales = keep.tile([P, S], U8, align_bytes=ALIGN)

        def first_layer(c, bank):
            cols = slice(c * CHUNK, (c + 1) * CHUNK)
            x_codes = x_codes_first[:] if c == 0 else x_codes_rest[:, (c - 1) * CHUNK : c * CHUNK]
            hidden = psum.tile([P, PACK, CHUNK], F32, tag=bank)
            for t in range(PACK):
                units = slice(t * P, (t + 1) * P)
                product(hidden[:, t, :], w1_codes[:, units], w1_scales[:, units], x_codes, x_scales[:, cols])
            nc.scalar.activation(h_grouped[c][:], hidden[:].rearrange("p t s -> p s t"), SILU)

        def quantize_h(c):
            cols = slice(c * CHUNK, (c + 1) * CHUNK)
            quantize(h_codes[:, cols], h_scales[:, cols], h_grouped[c][:].rearrange("p s t -> p (s t)"))

        def second_layer(b, lo, hi, bank):
            rows = slice(b * P, (b + 1) * P)
            acc = psum.tile([P, hi - lo], F32, tag=bank)
            product(acc[:], w2_codes[:, rows], w2_scales[:, rows], h_codes[:, lo:hi], h_scales[:, lo:hi])
            nc.scalar.copy(y_rows[b][:, lo:hi], acc[:])

        def scatter(b, lo, hi):
            nc.vector.tensor_tensor(windows[b][:].indirect(entries(lo, hi)), y_rows[b][:, lo:hi], gate_picked[:, lo:hi], MULT)

        quantize_w2(0)
        first_layer(0, "bank0")
        first_layer(1, "bank1")
        quantize_w2(1)
        quantize_h(0)
        second_layer(0, 0, CHUNK, "bank2")
        second_layer(1, 0, CHUNK, "bank3")
        quantize_h(1)
        scatter(0, 0, CHUNK)
        first_layer(2, "bank2")
        second_layer(0, CHUNK, 2 * CHUNK, "bank4")
        scatter(1, 0, CHUNK)
        quantize_h(2)
        first_layer(3, "bank3")
        scatter(0, CHUNK, 2 * CHUNK)
        quantize_h(3)
        second_layer(1, CHUNK, 2 * CHUNK, "bank5")
        second_layer(0, 2 * CHUNK, S, "bank0")
        second_layer(1, 2 * CHUNK, S, "bank1")
        scatter(1, CHUNK, 2 * CHUNK)
        scatter(0, 2 * CHUNK, S)
        nc.sync.dma_start(out=out[0:P, :], in_=windows[0][:])
        scatter(1, 2 * CHUNK, S)
        nc.sync.dma_start(out=out[P : 2 * P, :], in_=windows[1][:])
